import numpy as np
import ml_dtypes


def mxq(x, axis, fmt="e4m3"):
    dtype, down = {"e4m3": (ml_dtypes.float8_e4m3fn, 7), "e5m2": (ml_dtypes.float8_e5m2, 14)}[fmt]
    v = np.moveaxis(np.asarray(x, np.float32).astype(ml_dtypes.bfloat16).astype(np.float64), axis, -1)
    blocks = v.reshape(v.shape[:-1] + (-1, 32))
    amax = np.abs(blocks).max(-1, keepdims=True)
    byte = np.maximum(np.where(amax > 0, np.frexp(amax)[1] - 1 + 127, 0) - down, 1)
    scale = np.exp2(byte - 127.0)
    codes = (blocks / scale).astype(np.float32).astype(dtype).astype(np.float64)
    return np.moveaxis((codes * scale).reshape(v.shape), -1, axis)


WIDE = False


def mx_kscale(k):
    if not WIDE:
        return np.ones(k)
    levels = np.array([10, -10, 5, -5, 0])
    if k % 512:
        return np.exp2(np.random.permutation(np.resize(levels, k // 32))).repeat(32)
    a = np.empty((k // 512, 16))
    for p in range(k // 512):
        a[p, :8] = np.random.permutation(np.resize(levels, 8))
        for g in range(8):
            far = levels[np.abs(levels - a[p, g]) >= 10]
            a[p, g + 8] = far[np.random.randint(len(far))]
    return np.exp2(a.ravel()).repeat(32)


def f64(x):
    return np.asarray(x).astype(np.float64)


def striped(idx):
    return np.tile(idx.reshape(-1, 16).T, (8, 1)).astype(np.uint16)


def unstriped(offs):
    return offs[:16].T.reshape(-1).astype(np.int64)


def striped8(idx):
    return np.concatenate([x.reshape(-1, 16).T for x in idx]).astype(np.uint16)


def runs(offs, k):
    lists = np.stack([offs[16 * r : 16 * r + 16].T.reshape(-1) for r in range(8)]).astype(np.int64)
    return lists[np.arange(k) % 512 // 64]


def pack_weight(w):
    k, n = w.shape
    w = f64(np.asarray(w, np.float32).astype(ml_dtypes.bfloat16)).reshape(k // 32, 32, n)
    amax = np.abs(w).max(1)
    byte = np.clip(np.where(amax > 0, np.frexp(amax)[1] - 1 + 127 - 7, 1), 1, 254)
    scaled = (w * np.exp2(127.0 - byte)[:, None, :]).reshape(k, n).astype(np.float32)
    words = np.ascontiguousarray(scaled.reshape(k // 512, 128, 4, n).transpose(0, 1, 3, 2)).astype(ml_dtypes.float8_e4m3fn).view(np.uint8)
    return words, np.ascontiguousarray(byte.astype(np.uint8).reshape(k // 512, 16, n))


def unpack_weight(words, scales):
    g, p, n, _ = words.shape
    vals = np.ascontiguousarray(words).view(ml_dtypes.float8_e4m3fn).astype(np.float64) * np.repeat(np.exp2(scales.astype(np.float64) - 127.0), 8, axis=1)[..., None]
    return vals.transpose(0, 1, 3, 2).reshape(g * 512, n)


E2M1 = np.array([0.0, 0.5, 1.0, 1.5, 2.0, 3.0, 4.0, 6.0, -0.0, -0.5, -1.0, -1.5, -2.0, -3.0, -4.0, -6.0])


def pack_fp4(w):
    k, n = w.shape
    w = f64(np.asarray(w, np.float32).astype(ml_dtypes.bfloat16)).reshape(k // 32, 32, n)
    amax = np.abs(w).max(1)
    mant, ex = np.frexp(amax / 6.0)
    byte = np.clip(np.where(amax > 0, np.where(mant > 0.5, ex, ex - 1) + 127, 1), 1, 254)
    scaled = (w * np.exp2(127.0 - byte)[:, None, :]).reshape(k, n).astype(np.float32)
    c = np.ascontiguousarray(scaled.reshape(k // 512, 128, 4, n).transpose(0, 1, 3, 2)).astype(ml_dtypes.float4_e2m1fn).view(np.uint8) & 0xF
    words = (c[..., 0::2] | (c[..., 1::2] << 4)).reshape(k // 512, 128, 2 * n)
    return np.ascontiguousarray(words), np.ascontiguousarray(byte.astype(np.uint8).reshape(k // 512, 16, n))


def unpack_fp4(words, scales):
    g, _, n = scales.shape
    words = np.ascontiguousarray(words).reshape(g, 128, n, 2)
    nib = np.empty((g, 128, n, 4), np.uint8)
    nib[..., 0::2] = words & 0xF
    nib[..., 1::2] = words >> 4
    vals = E2M1[nib] * np.repeat(np.exp2(scales.astype(np.float64) - 127.0), 8, axis=1)[..., None]
    return vals.transpose(0, 1, 3, 2).reshape(g * 512, n)


def planes(y):
    n, m = y.shape
    v = y.astype(np.float32).astype(ml_dtypes.bfloat16).astype(np.float64).reshape(n // 32, 32, m)
    top = np.abs(v).max(1)
    byte = np.clip(np.where(top > 0, np.frexp(top)[1] - 1 + 127 - 7, 1), 1, 254)
    codes = (v * np.exp2(127.0 - byte)[:, None, :]).reshape(n, m).astype(np.float32).astype(ml_dtypes.float8_e4m3fn).view(np.uint8)
    words = codes.reshape(n // 512, 128, 4, m).transpose(0, 1, 3, 2)
    return np.ascontiguousarray(words), np.ascontiguousarray(byte.astype(np.uint8).reshape(n // 512, 16, m))


K, T, S, N, G, H, W = 512, 1024, 512, 512, 2048, 512, 256


def setup_inputs():
    n = np.random.standard_normal
    s = mx_kscale(K)[:, None]
    u = mx_kscale(S)
    packed_xT = pack_weight(n((K, T)) * s)
    packed_dT = pack_weight(n((K, G)) / s)
    packed_w1 = pack_fp4(n((H, N)) / np.sqrt(2 * H) / u[:, None])
    packed_w2 = pack_fp4(n((H, N)) / np.sqrt(2 * H) / u[:, None])
    perm = np.stack([np.random.permutation(S) for _ in range(8)])
    return {
        "x_words": packed_xT[0],
        "x_scales": packed_xT[1],
        "d_words": packed_dT[0],
        "d_scales": packed_dT[1],
        "gn": (np.random.uniform(0.5, 1.5, (H, 1)) * u[:, None]).astype(np.float32),
        "gm": (np.random.uniform(0.5, 1.5, (H, 1)) * u[:, None]).astype(np.float32),
        "w1_words": packed_w1[0],
        "w1_scales": packed_w1[1],
        "w2_words": packed_w2[0],
        "w2_scales": packed_w2[1],
        "offs": striped(np.random.permutation(T)[:S]),
        "k1": striped8(np.random.randint(0, G, (8, H))),
        "two": striped(np.random.permutation(T)[:S]),
        "k2": striped8(np.random.randint(0, G, (8, H))),
        "n1": striped(np.random.permutation(S)),
        "n2": striped(np.random.permutation(S)),
        "n3": striped(np.random.permutation(S)),
        "n4": striped8(perm[:, :W]),
        "n5": striped8(perm[:, W:]),
        "n6": striped(np.random.permutation(S)),
        "n7": striped(np.random.permutation(S)),
    }


def reference(x_words, x_scales, d_words, d_scales, gn, gm, w1_words, w1_scales, w2_words, w2_scales, offs, k1, two, k2, n1, n2, n3, n4, n5, n6, n7):
    d_k1 = unpack_weight(d_words, d_scales)[np.arange(K)[:, None], runs(k1, K)]
    xq = unpack_weight(x_words, x_scales)[:, unstriped(offs)]
    a = 0.0625 * (d_k1.T @ xq)
    st = a - a[:, unstriped(n1)]
    su = np.maximum(st, st[:, unstriped(n2)])
    z = f64(gn) * (su + 0.5 * su[:, unstriped(n3)])
    d_k2 = unpack_weight(d_words, d_scales)[np.arange(K)[:, None], runs(k2, K)]
    x_two = unpack_weight(x_words, x_scales)[:, unstriped(two)]
    b = 0.0625 * (d_k2.T @ x_two)
    pb = b[np.arange(H)[:, None], runs(n5, H)]
    pa = b[np.arange(H)[:, None], runs(n4, H)]
    rb = pb - (0.5 * pa)
    ra = np.sqrt((pa) ** 2 + (pb) ** 2 + 0.25)
    ds = np.zeros((H, S))
    ds[np.arange(H)[:, None], runs(n4, H)] = ra
    dt = ds.copy()
    dt[np.arange(H)[:, None], runs(n5, H)] = rb
    z2 = f64(gm) * dt
    h = unpack_fp4(w1_words, w1_scales).T @ mxq(z, 0, "e4m3") + unpack_fp4(w2_words, w2_scales).T @ mxq(z2, 0, "e4m3")
    out_0 = h * (h[:, unstriped(n6)] - h[:, unstriped(n7)])
    return (out_0,) + planes(out_0)

@@ -1,0 +1,292 @@
+from contextlib import ExitStack
+
+import concourse.mybir as mybir
+
+F32 = mybir.dt.float32
+BF16 = mybir.dt.bfloat16
+I32 = mybir.dt.int32
+U32 = mybir.dt.uint32
+U16 = mybir.dt.uint16
+U8 = mybir.dt.uint8
+FP8X4 = mybir.dt.float8_e4m3fn_x4
+FP4X4 = mybir.dt.float4_e2m1fn_x4
+ALU = mybir.AluOpType
+ACT = mybir.ActivationFunctionType
+
+P = 128
+PACK = 4
+S = 512
+HALF = S // 2
+PAD = 8
+T = 1024
+G = 2048
+
+FLOPS = 4 * 2 * 512 * 512 * 512
+
+
+def tile_picked_pqjthreepolarwind_none_po_kernel(
+    tc, x_words, x_scales, d_words, d_scales, gn, gm, w1_words, w1_scales, w2_words, w2_scales,
+    offs, k1, two, k2, n1, n2, n3, n4, n5, n6, n7, out_0, out_1, out_2,
+):
+    nc = tc.nc
+    with ExitStack() as ctx:
+        keep = ctx.enter_context(tc.tile_pool(name="keep", bufs=1))
+        psum = ctx.enter_context(tc.psum_pool(name="psum", bufs=1))
+
+        def sb(name, cols, dtype):
+            return keep.tile([P, cols], dtype, name=name, align_bytes=64)
+
+        lists = {}
+
+        def load_list(name, src):
+            lists[name] = keep.tile([P, src.shape[1]], U16, name="list_" + name)
+            nc.sync.dma_start(lists[name][:], src)
+
+        d_bytes = sb("d_bytes", G, U8)
+        x_bytes = sb("x_bytes", T, U8)
+        load_list("k2", k2)
+        nc.sync.dma_start(d_bytes[:].bitcast(I32), d_scales[0].bitcast(I32).unsqueeze(1).to_broadcast([16, 8, G // 4]))
+        load_list("two", two)
+        nc.sync.dma_start(x_bytes[:].bitcast(I32), x_scales[0].bitcast(I32).unsqueeze(1).to_broadcast([16, 8, T // 4]))
+        x_table = sb("x_table", T, I32)
+        d_table = sb("d_table", G, I32)
+        nc.sync.dma_start(x_table[:], x_words[0].rearrange("p n r -> p (n r)").bitcast(I32))
+        nc.sync.dma_start(d_table[:], d_words[0].rearrange("p n r -> p (n r)").bitcast(I32))
+        for name, src in (("n4", n4), ("n5", n5), ("k1", k1), ("offs", offs), ("n1", n1), ("n2", n2), ("n3", n3), ("n6", n6), ("n7", n7)):
+            load_list(name, src)
+
+        gains = {}
+        for name, src in (("gm", gm), ("gn", gn)):
+            gains[name] = sb(name, PACK, F32)
+            nc.gpsimd.dma_start(gains[name][:], src.rearrange("(p t) o -> p (t o)", t=PACK))
+
+        planes = {}
+        for br in ("b", "a", "w"):
+            planes[br] = sb("plane_" + br, 2 * S, U8)
+            nc.gpsimd.memset(planes[br][:], 0)
+
+        def padded(name):
+            tile = sb(name, S + PAD, F32)
+            nc.gpsimd.memset(tile[:, S:], 0.0)
+            return tile
+
+        a_rows = [padded("a%d" % t) for t in range(PACK)]
+        st_rows = [padded("st%d" % t) for t in range(PACK)]
+
+        def pick_bytes(br, d_list, x_list):
+            d_picked = sb("d_picked_bytes_" + br, S, U8)
+            x_picked = sb("x_picked_bytes_" + br, S, U8)
+            staged = sb("staged_" + br, 2 * S, U8)
+            nc.vector.tensor_copy(d_picked[:], d_bytes[:].indirect(lists[d_list][:]))
+            nc.vector.tensor_copy(x_picked[:], x_bytes[:].indirect(lists[x_list][:]))
+            nc.vector.tensor_copy(
+                staged[:, :S].rearrange("p (t m) -> p m t", t=PACK), d_picked[:].rearrange("p (m t) -> p m t", t=PACK)
+            )
+            nc.vector.tensor_copy(staged[:, S:].bitcast(I32), x_picked[:].bitcast(I32))
+            for i in range(4):
+                nc.sync.dma_start(planes[br][i:P:32, :].bitcast(I32), staged[8 * i : P : 32, :].bitcast(I32))
+
+        def pick_words(br, d_list, x_list):
+            x_picked = sb("x_picked_" + br, S, U32)
+            d_picked = sb("d_picked_" + br, S, U32)
+            d_dealt = sb("d_dealt_" + br, S, U32)
+            nc.vector.tensor_copy(d_picked[:], d_table[:].bitcast(U32).indirect(lists[d_list][:]))
+            nc.vector.tensor_copy(x_picked[:], x_table[:].bitcast(U32).indirect(lists[x_list][:]))
+            nc.vector.tensor_copy(
+                d_dealt[:].bitcast(I32).rearrange("p (t m) -> p m t", t=PACK),
+                d_picked[:].bitcast(I32).rearrange("p (m t) -> p m t", t=PACK),
+            )
+            banks = []
+            for t in range(PACK):
+                bank = psum.tile([P, S], F32, name="bank_%s%d" % (br, t), tag="bank_%s%d" % (br, t))
+                cols = slice(P * t, P * (t + 1))
+                nc.tensor.matmul_mx(
+                    out=bank[:], lhsT=d_dealt[:, cols].bitcast(FP8X4), lhsT_scale=planes[br][:, cols],
+                    rhs=x_picked[:].bitcast(FP8X4), rhs_scale=planes[br][:, S:], start=True, stop=True,
+                )
+                banks.append(bank)
+            return banks
+
+        pick_bytes("b", "k2", "two")
+        b_banks = pick_words("b", "k2", "two")
+        pick_bytes("a", "k1", "offs")
+        a_banks = pick_words("a", "k1", "offs")
+
+        w_words, w_bytes, w_raw, w_raw_bytes = {}, {}, {}, {}
+        w_table = keep.tile([P, G], U8, name="w_table", tag="d_bytes", align_bytes=64)
+        w_table_bytes = keep.tile([P, T], U8, name="w_table_bytes", tag="x_bytes", align_bytes=64)
+        for k, (name, words, scales) in enumerate((("w2", w2_words, w2_scales), ("w1", w1_words, w1_scales))):
+            w_raw[name] = w_table[:, 2 * S * k : 2 * S * (k + 1)]
+            w_raw_bytes[name] = w_table_bytes[:, S * k : S * (k + 1)]
+            nc.sync.dma_start(w_raw[name].bitcast(I32), words[0].bitcast(I32))
+            nc.sync.dma_start(
+                w_raw_bytes[name].bitcast(I32), scales[0].bitcast(I32).unsqueeze(1).to_broadcast([16, 8, S // 4])
+            )
+        w_staged = sb("staged_w", 2 * S, U8)
+        for k, name in enumerate(("w2", "w1")):
+            w_words[name] = sb(name + "_dealt", 2 * S, U8)
+            w_bytes[name] = planes["w"][:, S * k : S * (k + 1)]
+            nc.vector.tensor_copy(
+                w_words[name][:].rearrange("p (t m e) -> p m t e", t=PACK, e=2),
+                w_raw[name][:].rearrange("p (m t e) -> p m t e", t=PACK, e=2),
+            )
+            nc.vector.tensor_copy(
+                w_staged[:, S * k : S * (k + 1)].rearrange("p (t m) -> p m t", t=PACK),
+                w_raw_bytes[name][:].rearrange("p (m t) -> p m t", t=PACK),
+            )
+        for i in range(4):
+            nc.sync.dma_start(planes["w"][i:P:32, :].bitcast(I32), w_staged[8 * i : P : 32, :].bitcast(I32))
+
+        z2_rows = keep.tile([P, PACK, S], BF16, name="z2_rows", align_bytes=64)
+        pair = [sb("pair%d" % t, S, F32) for t in range(PACK)]
+        radius2 = [sb("radius2_%d" % t, HALF, F32) for t in range(PACK)]
+        dt = [sb("dt%d" % t, S, F32) for t in range(PACK)]
+        gained = [sb("gained%d" % t, S, F32) for t in range(PACK)]
+        h_rows = [sb("h%d" % t, S, F32) for t in range(PACK)]
+        z2_codes = sb("z2_codes", S, U32)
+        z2_bytes = sb("z2_bytes", S, U8)
+        z_rows = [keep.tile([P, PACK, HALF], BF16, name="z_rows%d" % c, align_bytes=64) for c in range(2)]
+
+        def fetch_pairs(t):
+            b_row = sb("b%d" % t, S, F32)
+            squares = sb("squares%d" % t, S, F32)
+            nc.scalar.activation(b_row[:], b_banks[t][:], ACT.Copy, scale=0.0625)
+            nc.scalar.activation(pair[t][:, :HALF], b_row[:].indirect(lists["n4"][:]), ACT.Copy, scale=-0.5)
+            nc.scalar.activation(pair[t][:, HALF:], b_row[:].indirect(lists["n5"][:]), ACT.Copy)
+            nc.scalar.activation(squares[:], pair[t][:], ACT.Square)
+            nc.vector.scalar_tensor_tensor(radius2[t][:], squares[:, :HALF], 4.0, squares[:, HALF:], ALU.mult, ALU.add)
+            nc.vector.tensor_tensor(dt[t][:].indirect(lists["n5"][:]), pair[t][:, HALF:], pair[t][:, :HALF], ALU.add)
+
+        def put_roots(t):
+            ra = sb("ra%d" % t, HALF, F32)
+            nc.scalar.activation(ra[:], radius2[t][:], ACT.Sqrt, bias=0.25)
+            nc.vector.tensor_copy(dt[t][:].indirect(lists["n4"][:]), ra[:])
+
+        def gain_z2(t):
+            nc.scalar.activation(z2_rows[:, t, :], dt[t][:], ACT.Copy, scale=gains["gm"][:, t : t + 1])
+
+        def quantise_z2():
+            z2_grouped = sb("z2_grouped", PACK * S, BF16)
+            nc.vector.tensor_copy(
+                z2_grouped[:].rearrange("p (j t) -> p j t", t=PACK), z2_rows[:].rearrange("p t j -> p j t")
+            )
+            nc.vector.quantize_mx(out=z2_codes[:].bitcast(FP8X4), scales=z2_bytes[:], in_=z2_grouped[:])
+
+        def less_first(t):
+            first = sb("first%d" % t, S, F32)
+            nc.scalar.activation(a_rows[t][:, :S], a_banks[t][:], ACT.Copy, scale=0.0625)
+            nc.scalar.activation(first[:], a_rows[t][:].indirect(lists["n1"][:]), ACT.Copy)
+            nc.vector.scalar_tensor_tensor(st_rows[t][:, :S], a_banks[t][:], 0.0625, first[:], ALU.mult, ALU.subtract)
+
+        def larger_of_second(t):
+            second = sb("second%d" % t, S, F32)
+            su = sb("su%d" % t, S, F32)
+            nc.scalar.activation(second[:], st_rows[t][:].indirect(lists["n2"][:]), ACT.Copy)
+            nc.vector.tensor_tensor(su[:], st_rows[t][:, :S], second[:], ALU.max)
+            nc.vector.tensor_scalar(gained[t][:], su[:], gains["gn"][:, t : t + 1], None, ALU.mult)
+
+        def plus_third(c, t):
+            third = sb("third%d_%d" % (t, c), HALF, F32)
+            nc.scalar.activation(third[:], gained[t][:].indirect(lists["n3"][:, 16 * c : 16 * (c + 1)]), ACT.Copy)
+            nc.vector.scalar_tensor_tensor(
+                z_rows[c][:, t, :], third[:], 0.5, gained[t][:, HALF * c : HALF * (c + 1)], ALU.mult, ALU.add
+            )
+
+        z_codes = [sb("z_codes%d" % c, HALF, U32) for c in range(2)]
+        z_bytes = [sb("z_bytes%d" % c, HALF, U8) for c in range(2)]
+
+        def quantise_z(c):
+            z_grouped = sb("z_grouped%d" % c, PACK * HALF, BF16)
+            nc.vector.tensor_copy(
+                z_grouped[:].rearrange("p (j t) -> p j t", t=PACK), z_rows[c][:].rearrange("p t j -> p j t")
+            )
+            nc.vector.quantize_mx(out=z_codes[c][:].bitcast(FP8X4), scales=z_bytes[c][:], in_=z_grouped[:])
+
+        def sum_h(c):
+            cols = slice(HALF * c, HALF * (c + 1))
+            banks = [
+                psum.tile([P, HALF], F32, name="bank_h%d_%d" % (t, c), tag="bank_%s%d" % ("ba"[c], t)) for t in range(PACK)
+            ]
+            for name, codes, scale_bytes in (
+                ("w2", z2_codes[:, cols], z2_bytes[:, cols]), ("w1", z_codes[c][:], z_bytes[c][:])
+            ):
+                for t in range(PACK):
+                    nc.tensor.matmul_mx(
+                        out=banks[t][:], lhsT=w_words[name][:, 2 * P * t : 2 * P * (t + 1)].bitcast(FP4X4),
+                        lhsT_scale=w_bytes[name][:, P * t : P * (t + 1)],
+                        rhs=codes.bitcast(FP8X4), rhs_scale=scale_bytes, start=(name == "w2"), stop=(name == "w1"),
+                    )
+            for t in range(PACK):
+                if c == 0 or t % 2 == 0:
+                    nc.scalar.copy(h_rows[t][:, cols], banks[t][:])
+                else:
+                    nc.vector.tensor_copy(h_rows[t][:, cols], banks[t][:])
+
+        fetch_pairs(0)
+        fetch_pairs(1)
+        fetch_pairs(2)
+        less_first(0)
+        put_roots(0)
+        put_roots(1)
+        less_first(1)
+        less_first(2)
+        put_roots(2)
+        less_first(3)
+        fetch_pairs(3)
+        larger_of_second(0)
+        gain_z2(0)
+        larger_of_second(1)
+        put_roots(3)
+        gain_z2(1)
+        larger_of_second(2)
+        larger_of_second(3)
+        gain_z2(2)
+        plus_third(0, 0)
+        plus_third(0, 1)
+        gain_z2(3)
+        plus_third(0, 2)
+        plus_third(0, 3)
+        quantise_z2()
+        quantise_z(0)
+        plus_third(1, 0)
+        plus_third(1, 1)
+        sum_h(0)
+        plus_third(1, 2)
+        plus_third(1, 3)
+        quantise_z(1)
+        sum_h(1)
+        out_rows = out_0.rearrange("(p t) j -> p t j", t=PACK)
+        out_words = out_1[0].rearrange("p n r -> p (n r)").bitcast(I32)
+        y_bytes = sb("y_bytes", S, U8)
+        for c, (lo, hi) in enumerate(((0, 256), (256, 512))):
+            cols = slice(lo, hi)
+            width = hi - lo
+            entries = slice(lo // 16, hi // 16)
+            y_rows = keep.tile([P, PACK, width], F32, name="y_rows%d" % c, align_bytes=64)
+            for t in range(PACK):
+                seventh = sb("seventh%d_%d" % (t, c), width, F32)
+                diff = sb("diff%d_%d" % (t, c), width, F32)
+                nc.scalar.activation(seventh[:], h_rows[t][:].indirect(lists["n7"][:, entries]), ACT.Copy)
+                if t % 2 == 1:
+                    nc.vector.tensor_tensor(diff[:], h_rows[t][:].indirect(lists["n6"][:, entries]), seventh[:], ALU.subtract)
+                else:
+                    sixth = sb("sixth%d_%d" % (t, c), width, F32)
+                    nc.scalar.activation(sixth[:], h_rows[t][:].indirect(lists["n6"][:, entries]), ACT.Copy)
+                    nc.vector.tensor_tensor(diff[:], sixth[:], seventh[:], ALU.subtract)
+                nc.vector.tensor_tensor(y_rows[:, t, :], diff[:], h_rows[t][:, cols], ALU.mult)
+            nc.sync.dma_start(out_rows[:, :, cols], y_rows[:])
+            y_grouped = sb("y_grouped%d" % c, PACK * width, BF16)
+            y_codes = sb("y_codes%d" % c, width, U32)
+            if c == 0:
+                nc.scalar.copy(
+                    y_grouped[:].rearrange("p (j t) -> p j t", t=PACK), y_rows[:].rearrange("p t j -> p j t")
+                )
+            else:
+                nc.vector.tensor_copy(
+                    y_grouped[:].rearrange("p (j t) -> p j t", t=PACK), y_rows[:].rearrange("p t j -> p j t")
+                )
+            nc.vector.quantize_mx(out=y_codes[:].bitcast(FP8X4), scales=y_bytes[:, cols], in_=y_grouped[:])
+            nc.sync.dma_start(out_words[:, cols], y_codes[:].bitcast(I32))
+        for q in range(4):
+            queue = nc.sync if q % 2 == 0 else nc.scalar
+            queue.dma_start(out_2[0, 4 * q : 4 * q + 4, :].bitcast(I32), y_bytes[32 * q : 32 * q + 4, :].bitcast(I32))

@@ -21,6 +21,14 @@ PAD = 8
 T = 1024
 G = 2048
 
+Z_PIECES = ((0, 256), (256, 512))
+Y_PIECES = ((0,384),(384,512))
+SIXTH_ON_SCALAR = ((0,3),(1,0),(1,1),(1,2),(1,3))
+GAIN_ON_SCALAR = ()
+Z2_SCALAR_COLS = 256
+Y_GROUP_ON_SCALAR = (0,)
+H_ON_VECTOR = ((1, 1), (1, 3))
+
 FLOPS = 4 * 2 * 512 * 512 * 512
 
 
@@ -50,24 +58,23 @@ def tile_picked_pqjthreepolarwind_none_po_kernel(
         nc.sync.dma_start(x_bytes[:].bitcast(I32), x_scales[0].bitcast(I32).unsqueeze(1).to_broadcast([16, 8, T // 4]))
         x_table = sb("x_table", T, I32)
         d_table = sb("d_table", G, I32)
-        nc.sync.dma_start(x_table[:], x_words[0].rearrange("p n r -> p (n r)").bitcast(I32))
         nc.sync.dma_start(d_table[:], d_words[0].rearrange("p n r -> p (n r)").bitcast(I32))
+        nc.sync.dma_start(x_table[:], x_words[0].rearrange("p n r -> p (n r)").bitcast(I32))
         for name, src in (("n4", n4), ("n5", n5), ("k1", k1), ("offs", offs), ("n1", n1), ("n2", n2), ("n3", n3), ("n6", n6), ("n7", n7)):
             load_list(name, src)
 
-        gains = {}
-        for name, src in (("gm", gm), ("gn", gn)):
-            gains[name] = sb(name, PACK, F32)
-            nc.gpsimd.dma_start(gains[name][:], src.rearrange("(p t) o -> p (t o)", t=PACK))
+        warm = sb("warm", 2, F32)
+        nc.vector.memset(warm[:, :1], 1.0)
+        nc.scalar.activation(warm[:, 1:], warm[:, :1], ACT.Sqrt)
 
         planes = {}
         for br in ("b", "a", "w"):
             planes[br] = sb("plane_" + br, 2 * S, U8)
-            nc.gpsimd.memset(planes[br][:], 0)
+            nc.vector.memset(planes[br][:].bitcast(I32), 0)
 
         def padded(name):
             tile = sb(name, S + PAD, F32)
-            nc.gpsimd.memset(tile[:, S:], 0.0)
+            nc.vector.memset(tile[:, S:], 0.0)
             return tile
 
         a_rows = [padded("a%d" % t) for t in range(PACK)]
@@ -80,7 +87,7 @@ def tile_picked_pqjthreepolarwind_none_po_kernel(
             nc.vector.tensor_copy(d_picked[:], d_bytes[:].indirect(lists[d_list][:]))
             nc.vector.tensor_copy(x_picked[:], x_bytes[:].indirect(lists[x_list][:]))
             nc.vector.tensor_copy(
-                staged[:, :S].rearrange("p (t m) -> p m t", t=PACK), d_picked[:].rearrange("p (m t) -> p m t", t=PACK)
+                staged[:, :S].rearrange("p (t m) -> p t m", t=PACK), d_picked[:].rearrange("p (m t) -> p t m", t=PACK)
             )
             nc.vector.tensor_copy(staged[:, S:].bitcast(I32), x_picked[:].bitcast(I32))
             for i in range(4):
@@ -93,8 +100,8 @@ def tile_picked_pqjthreepolarwind_none_po_kernel(
             nc.vector.tensor_copy(d_picked[:], d_table[:].bitcast(U32).indirect(lists[d_list][:]))
             nc.vector.tensor_copy(x_picked[:], x_table[:].bitcast(U32).indirect(lists[x_list][:]))
             nc.vector.tensor_copy(
-                d_dealt[:].bitcast(I32).rearrange("p (t m) -> p m t", t=PACK),
-                d_picked[:].bitcast(I32).rearrange("p (m t) -> p m t", t=PACK),
+                d_dealt[:].bitcast(I32).rearrange("p (t g m) -> p g t m", t=PACK, m=4),
+                d_picked[:].bitcast(I32).rearrange("p (g m t) -> p g t m", t=PACK, m=4),
             )
             banks = []
             for t in range(PACK):
@@ -112,6 +119,11 @@ def tile_picked_pqjthreepolarwind_none_po_kernel(
         pick_bytes("a", "k1", "offs")
         a_banks = pick_words("a", "k1", "offs")
 
+        gains = {}
+        for name, src, br in (("gm", gm, "b"), ("gn", gn, "a")):
+            gains[name] = keep.tile([P, PACK], F32, name=name, tag="staged_" + br, align_bytes=64)
+            nc.sync.dma_start(gains[name][:], src.rearrange("(p t) o -> p (t o)", t=PACK))
+
         w_words, w_bytes, w_raw, w_raw_bytes = {}, {}, {}, {}
         w_table = keep.tile([P, G], U8, name="w_table", tag="d_bytes", align_bytes=64)
         w_table_bytes = keep.tile([P, T], U8, name="w_table_bytes", tag="x_bytes", align_bytes=64)
@@ -127,12 +139,12 @@ def tile_picked_pqjthreepolarwind_none_po_kernel(
             w_words[name] = sb(name + "_dealt", 2 * S, U8)
             w_bytes[name] = planes["w"][:, S * k : S * (k + 1)]
             nc.vector.tensor_copy(
-                w_words[name][:].rearrange("p (t m e) -> p m t e", t=PACK, e=2),
-                w_raw[name][:].rearrange("p (m t e) -> p m t e", t=PACK, e=2),
+                w_words[name][:].rearrange("p (t m e) -> p t m e", t=PACK, e=2),
+                w_raw[name][:].rearrange("p (m t e) -> p t m e", t=PACK, e=2),
             )
             nc.vector.tensor_copy(
-                w_staged[:, S * k : S * (k + 1)].rearrange("p (t m) -> p m t", t=PACK),
-                w_raw_bytes[name][:].rearrange("p (m t) -> p m t", t=PACK),
+                w_staged[:, S * k : S * (k + 1)].rearrange("p (t m) -> p t m", t=PACK),
+                w_raw_bytes[name][:].rearrange("p (m t) -> p t m", t=PACK),
             )
         for i in range(4):
             nc.sync.dma_start(planes["w"][i:P:32, :].bitcast(I32), w_staged[8 * i : P : 32, :].bitcast(I32))
@@ -141,11 +153,10 @@ def tile_picked_pqjthreepolarwind_none_po_kernel(
         pair = [sb("pair%d" % t, S, F32) for t in range(PACK)]
         radius2 = [sb("radius2_%d" % t, HALF, F32) for t in range(PACK)]
         dt = [sb("dt%d" % t, S, F32) for t in range(PACK)]
-        gained = [sb("gained%d" % t, S, F32) for t in range(PACK)]
+        gained = keep.tile([P, PACK, S], F32, name="gained", align_bytes=64)
         h_rows = [sb("h%d" % t, S, F32) for t in range(PACK)]
         z2_codes = sb("z2_codes", S, U32)
         z2_bytes = sb("z2_bytes", S, U8)
-        z_rows = [keep.tile([P, PACK, HALF], BF16, name="z_rows%d" % c, align_bytes=64) for c in range(2)]
 
         def fetch_pairs(t):
             b_row = sb("b%d" % t, S, F32)
@@ -167,9 +178,13 @@ def tile_picked_pqjthreepolarwind_none_po_kernel(
 
         def quantise_z2():
             z2_grouped = sb("z2_grouped", PACK * S, BF16)
-            nc.vector.tensor_copy(
-                z2_grouped[:].rearrange("p (j t) -> p j t", t=PACK), z2_rows[:].rearrange("p t j -> p j t")
-            )
+            dst = z2_grouped[:].rearrange("p (g j t) -> p g t j", t=PACK, j=4)
+            src = z2_rows[:].rearrange("p t (g j) -> p g t j", j=4)
+            cut = Z2_SCALAR_COLS // 4
+            if cut:
+                nc.scalar.copy(dst[:, :cut], src[:, :cut])
+            if cut < S // 4:
+                nc.vector.tensor_copy(dst[:, cut:], src[:, cut:])
             nc.vector.quantize_mx(out=z2_codes[:].bitcast(FP8X4), scales=z2_bytes[:], in_=z2_grouped[:])
 
         def less_first(t):
@@ -183,32 +198,39 @@ def tile_picked_pqjthreepolarwind_none_po_kernel(
             su = sb("su%d" % t, S, F32)
             nc.scalar.activation(second[:], st_rows[t][:].indirect(lists["n2"][:]), ACT.Copy)
             nc.vector.tensor_tensor(su[:], st_rows[t][:, :S], second[:], ALU.max)
-            nc.vector.tensor_scalar(gained[t][:], su[:], gains["gn"][:, t : t + 1], None, ALU.mult)
+            if t in GAIN_ON_SCALAR:
+                nc.scalar.activation(gained[:, t, :], su[:], ACT.Copy, scale=gains["gn"][:, t : t + 1])
+            else:
+                nc.vector.tensor_scalar(gained[:, t, :], su[:], gains["gn"][:, t : t + 1], None, ALU.mult)
 
-        def plus_third(c, t):
-            third = sb("third%d_%d" % (t, c), HALF, F32)
-            nc.scalar.activation(third[:], gained[t][:].indirect(lists["n3"][:, 16 * c : 16 * (c + 1)]), ACT.Copy)
-            nc.vector.scalar_tensor_tensor(
-                z_rows[c][:, t, :], third[:], 0.5, gained[t][:, HALF * c : HALF * (c + 1)], ALU.mult, ALU.add
+        def make_z(c):
+            lo, hi = Z_PIECES[c]
+            width = hi - lo
+            third = keep.tile([P, PACK, width], F32, name="third%d" % c, align_bytes=64)
+            for t in range(PACK):
+                nc.scalar.activation(
+                    third[:, t, :], gained[:, t, :].indirect(lists["n3"][:, lo // 16 : hi // 16]), ACT.Copy, scale=0.5
+                )
+            z_grouped = sb("z_grouped%d" % c, PACK * width, BF16)
+            nc.vector.tensor_tensor(
+                z_grouped[:].rearrange("p (g j t) -> p g t j", t=PACK, j=4),
+                third[:].rearrange("p t (g j) -> p g t j", j=4),
+                gained[:, :, lo:hi].rearrange("p t (g j) -> p g t j", j=4),
+                ALU.add,
             )
+            z_codes = sb("z_codes%d" % c, width, U32)
+            z_bytes = sb("z_bytes%d" % c, width, U8)
+            nc.vector.quantize_mx(out=z_codes[:].bitcast(FP8X4), scales=z_bytes[:], in_=z_grouped[:])
+            return z_codes, z_bytes
 
-        z_codes = [sb("z_codes%d" % c, HALF, U32) for c in range(2)]
-        z_bytes = [sb("z_bytes%d" % c, HALF, U8) for c in range(2)]
-
-        def quantise_z(c):
-            z_grouped = sb("z_grouped%d" % c, PACK * HALF, BF16)
-            nc.vector.tensor_copy(
-                z_grouped[:].rearrange("p (j t) -> p j t", t=PACK), z_rows[c][:].rearrange("p t j -> p j t")
-            )
-            nc.vector.quantize_mx(out=z_codes[c][:].bitcast(FP8X4), scales=z_bytes[c][:], in_=z_grouped[:])
-
-        def sum_h(c):
-            cols = slice(HALF * c, HALF * (c + 1))
+        def sum_h(c, z_codes, z_bytes):
+            lo, hi = Z_PIECES[c]
+            cols = slice(lo, hi)
             banks = [
-                psum.tile([P, HALF], F32, name="bank_h%d_%d" % (t, c), tag="bank_%s%d" % ("ba"[c], t)) for t in range(PACK)
+                psum.tile([P, hi - lo], F32, name="bank_h%d_%d" % (t, c), tag="bank_%s%d" % ("ba"[c % 2], t)) for t in range(PACK)
             ]
             for name, codes, scale_bytes in (
-                ("w2", z2_codes[:, cols], z2_bytes[:, cols]), ("w1", z_codes[c][:], z_bytes[c][:])
+                ("w2", z2_codes[:, cols], z2_bytes[:, cols]), ("w1", z_codes[:], z_bytes[:])
             ):
                 for t in range(PACK):
                     nc.tensor.matmul_mx(
@@ -217,48 +239,26 @@ def tile_picked_pqjthreepolarwind_none_po_kernel(
                         rhs=codes.bitcast(FP8X4), rhs_scale=scale_bytes, start=(name == "w2"), stop=(name == "w1"),
                     )
             for t in range(PACK):
-                if c == 0 or t % 2 == 0:
-                    nc.scalar.copy(h_rows[t][:, cols], banks[t][:])
-                else:
+                if (c, t) in H_ON_VECTOR:
                     nc.vector.tensor_copy(h_rows[t][:, cols], banks[t][:])
+                else:
+                    nc.scalar.copy(h_rows[t][:, cols], banks[t][:])
 
-        fetch_pairs(0)
-        fetch_pairs(1)
-        fetch_pairs(2)
-        less_first(0)
-        put_roots(0)
-        put_roots(1)
-        less_first(1)
-        less_first(2)
-        put_roots(2)
-        less_first(3)
-        fetch_pairs(3)
-        larger_of_second(0)
-        gain_z2(0)
-        larger_of_second(1)
-        put_roots(3)
-        gain_z2(1)
-        larger_of_second(2)
-        larger_of_second(3)
-        gain_z2(2)
-        plus_third(0, 0)
-        plus_third(0, 1)
-        gain_z2(3)
-        plus_third(0, 2)
-        plus_third(0, 3)
+        for t in range(PACK):
+            fetch_pairs(t)
+        for t in range(PACK):
+            less_first(t)
+            put_roots(t)
+        for t in range(PACK):
+            larger_of_second(t)
+            gain_z2(t)
         quantise_z2()
-        quantise_z(0)
-        plus_third(1, 0)
-        plus_third(1, 1)
-        sum_h(0)
-        plus_third(1, 2)
-        plus_third(1, 3)
-        quantise_z(1)
-        sum_h(1)
+        for c in range(len(Z_PIECES)):
+            sum_h(c, *make_z(c))
         out_rows = out_0.rearrange("(p t) j -> p t j", t=PACK)
         out_words = out_1[0].rearrange("p n r -> p (n r)").bitcast(I32)
         y_bytes = sb("y_bytes", S, U8)
-        for c, (lo, hi) in enumerate(((0, 256), (256, 512))):
+        for c, (lo, hi) in enumerate(Y_PIECES):
             cols = slice(lo, hi)
             width = hi - lo
             entries = slice(lo // 16, hi // 16)
@@ -266,24 +266,24 @@ def tile_picked_pqjthreepolarwind_none_po_kernel(
             for t in range(PACK):
                 seventh = sb("seventh%d_%d" % (t, c), width, F32)
                 diff = sb("diff%d_%d" % (t, c), width, F32)
-                nc.scalar.activation(seventh[:], h_rows[t][:].indirect(lists["n7"][:, entries]), ACT.Copy)
-                if t % 2 == 1:
-                    nc.vector.tensor_tensor(diff[:], h_rows[t][:].indirect(lists["n6"][:, entries]), seventh[:], ALU.subtract)
+                nc.scalar.activation(seventh[:], h_rows[t][:].indirect(lists["n7"][:, entries]), ACT.Copy, scale=-1.0)
+                if (c, t) not in SIXTH_ON_SCALAR:
+                    nc.vector.tensor_tensor(diff[:], h_rows[t][:].indirect(lists["n6"][:, entries]), seventh[:], ALU.add)
                 else:
                     sixth = sb("sixth%d_%d" % (t, c), width, F32)
                     nc.scalar.activation(sixth[:], h_rows[t][:].indirect(lists["n6"][:, entries]), ACT.Copy)
-                    nc.vector.tensor_tensor(diff[:], sixth[:], seventh[:], ALU.subtract)
+                    nc.vector.tensor_tensor(diff[:], sixth[:], seventh[:], ALU.add)
                 nc.vector.tensor_tensor(y_rows[:, t, :], diff[:], h_rows[t][:, cols], ALU.mult)
             nc.sync.dma_start(out_rows[:, :, cols], y_rows[:])
             y_grouped = sb("y_grouped%d" % c, PACK * width, BF16)
             y_codes = sb("y_codes%d" % c, width, U32)
-            if c == 0:
+            if c in Y_GROUP_ON_SCALAR:
                 nc.scalar.copy(
-                    y_grouped[:].rearrange("p (j t) -> p j t", t=PACK), y_rows[:].rearrange("p t j -> p j t")
+                    y_grouped[:].rearrange("p (g j t) -> p g t j", t=PACK, j=4), y_rows[:].rearrange("p t (g j) -> p g t j", j=4)
                 )
             else:
                 nc.vector.tensor_copy(
-                    y_grouped[:].rearrange("p (j t) -> p j t", t=PACK), y_rows[:].rearrange("p t j -> p j t")
+                    y_grouped[:].rearrange("p (g j t) -> p g t j", t=PACK, j=4), y_rows[:].rearrange("p t (g j) -> p g t j", j=4)
                 )
             nc.vector.quantize_mx(out=y_codes[:].bitcast(FP8X4), scales=y_bytes[:, cols], in_=y_grouped[:])
             nc.sync.dma_start(out_words[:, cols], y_codes[:].bitcast(I32))

@@ -20,14 +20,14 @@ HALF = S // 2
 PAD = 8
 T = 1024
 G = 2048
+LIST_ROWS = 16
+LINE = 4
 
-Z_PIECES = ((0, 256), (256, 512))
-Y_PIECES = ((0,384),(384,512))
-SIXTH_ON_SCALAR = ((0,3),(1,0),(1,1),(1,2),(1,3))
-GAIN_ON_SCALAR = ()
-Z2_SCALAR_COLS = 256
-Y_GROUP_ON_SCALAR = (0,)
-H_ON_VECTOR = ((1, 1), (1, 3))
+Z_PIECES = ((0, HALF), (HALF, S))
+Y_PIECES = ((0, 384), (384, S))
+A_ORDER = (1, 2, 3, 0)
+GM_TILES_ON_SCALAR = 2
+Z2_COLUMNS_ON_SCALAR = 256
 
 FLOPS = 4 * 2 * 512 * 512 * 512
 
@@ -41,8 +41,25 @@ def tile_picked_pqjthreepolarwind_none_po_kernel(
         keep = ctx.enter_context(tc.tile_pool(name="keep", bufs=1))
         psum = ctx.enter_context(tc.psum_pool(name="psum", bufs=1))
 
-        def sb(name, cols, dtype):
-            return keep.tile([P, cols], dtype, name=name, align_bytes=64)
+        def sb(name, cols, dtype, tag=None):
+            return keep.tile([P, cols], dtype, name=name, tag=tag or name, align_bytes=64)
+
+        def sb_rows(name, cols, dtype):
+            return keep.tile([P, PACK, cols], dtype, name=name, align_bytes=64)
+
+        def grouped_view(tile):
+            return tile.rearrange("p (g j t) -> p g t j", t=PACK, j=LINE)
+
+        def rows_view(rows):
+            return rows.rearrange("p t (g j) -> p g t j", j=LINE)
+
+        def load_scale_rows(tile, scales):
+            rows = scales[0].bitcast(I32)
+            nc.sync.dma_start(tile.bitcast(I32), rows.unsqueeze(1).to_broadcast([16, 8, rows.shape[1]]))
+
+        def move_scale_rows(plane, staged):
+            for i in range(4):
+                nc.sync.dma_start(plane[i:P:32, :].bitcast(I32), staged[8 * i : P : 32, :].bitcast(I32))
 
         lists = {}
 
@@ -53,14 +70,17 @@ def tile_picked_pqjthreepolarwind_none_po_kernel(
         d_bytes = sb("d_bytes", G, U8)
         x_bytes = sb("x_bytes", T, U8)
         load_list("k2", k2)
-        nc.sync.dma_start(d_bytes[:].bitcast(I32), d_scales[0].bitcast(I32).unsqueeze(1).to_broadcast([16, 8, G // 4]))
+        load_scale_rows(d_bytes[:], d_scales)
         load_list("two", two)
-        nc.sync.dma_start(x_bytes[:].bitcast(I32), x_scales[0].bitcast(I32).unsqueeze(1).to_broadcast([16, 8, T // 4]))
+        load_scale_rows(x_bytes[:], x_scales)
         x_table = sb("x_table", T, I32)
         d_table = sb("d_table", G, I32)
         nc.sync.dma_start(d_table[:], d_words[0].rearrange("p n r -> p (n r)").bitcast(I32))
         nc.sync.dma_start(x_table[:], x_words[0].rearrange("p n r -> p (n r)").bitcast(I32))
-        for name, src in (("n4", n4), ("n5", n5), ("k1", k1), ("offs", offs), ("n1", n1), ("n2", n2), ("n3", n3), ("n6", n6), ("n7", n7)):
+        for name, src in (
+            ("n4", n4), ("n5", n5), ("k1", k1), ("offs", offs),
+            ("n1", n1), ("n2", n2), ("n3", n3), ("n6", n6), ("n7", n7),
+        ):
             load_list(name, src)
 
         warm = sb("warm", 2, F32)
@@ -68,9 +88,9 @@ def tile_picked_pqjthreepolarwind_none_po_kernel(
         nc.scalar.activation(warm[:, 1:], warm[:, :1], ACT.Sqrt)
 
         planes = {}
-        for br in ("b", "a", "w"):
-            planes[br] = sb("plane_" + br, 2 * S, U8)
-            nc.vector.memset(planes[br][:].bitcast(I32), 0)
+        for name in ("b", "a", "w"):
+            planes[name] = sb("plane_" + name, 2 * S, U8)
+            nc.vector.memset(planes[name][:].bitcast(I32), 0)
 
         def padded(name):
             tile = sb(name, S + PAD, F32)
@@ -80,83 +100,61 @@ def tile_picked_pqjthreepolarwind_none_po_kernel(
         a_rows = [padded("a%d" % t) for t in range(PACK)]
         st_rows = [padded("st%d" % t) for t in range(PACK)]
 
-        def pick_bytes(br, d_list, x_list):
-            d_picked = sb("d_picked_bytes_" + br, S, U8)
-            x_picked = sb("x_picked_bytes_" + br, S, U8)
-            staged = sb("staged_" + br, 2 * S, U8)
+        def pick_bytes(branch, d_list, x_list):
+            d_picked = sb("d_picked_bytes_" + branch, S, U8)
+            x_picked = sb("x_picked_bytes_" + branch, S, U8)
+            staged = sb("staged_" + branch, 2 * S, U8)
             nc.vector.tensor_copy(d_picked[:], d_bytes[:].indirect(lists[d_list][:]))
             nc.vector.tensor_copy(x_picked[:], x_bytes[:].indirect(lists[x_list][:]))
             nc.vector.tensor_copy(
                 staged[:, :S].rearrange("p (t m) -> p t m", t=PACK), d_picked[:].rearrange("p (m t) -> p t m", t=PACK)
             )
             nc.vector.tensor_copy(staged[:, S:].bitcast(I32), x_picked[:].bitcast(I32))
-            for i in range(4):
-                nc.sync.dma_start(planes[br][i:P:32, :].bitcast(I32), staged[8 * i : P : 32, :].bitcast(I32))
+            move_scale_rows(planes[branch], staged)
 
-        def pick_words(br, d_list, x_list):
-            x_picked = sb("x_picked_" + br, S, U32)
-            d_picked = sb("d_picked_" + br, S, U32)
-            d_dealt = sb("d_dealt_" + br, S, U32)
+        def pick_words_and_multiply(branch, d_list, x_list, tile_order):
+            x_picked = sb("x_picked_" + branch, S, U32)
+            d_picked = sb("d_picked_" + branch, S, U32)
+            d_dealt = sb("d_dealt_" + branch, S, U32)
             nc.vector.tensor_copy(d_picked[:], d_table[:].bitcast(U32).indirect(lists[d_list][:]))
             nc.vector.tensor_copy(x_picked[:], x_table[:].bitcast(U32).indirect(lists[x_list][:]))
             nc.vector.tensor_copy(
-                d_dealt[:].bitcast(I32).rearrange("p (t g m) -> p g t m", t=PACK, m=4),
-                d_picked[:].bitcast(I32).rearrange("p (g m t) -> p g t m", t=PACK, m=4),
+                d_dealt[:].bitcast(I32).rearrange("p (t g m) -> p g t m", t=PACK, m=LINE),
+                d_picked[:].bitcast(I32).rearrange("p (g m t) -> p g t m", t=PACK, m=LINE),
             )
-            banks = []
-            for t in range(PACK):
-                bank = psum.tile([P, S], F32, name="bank_%s%d" % (br, t), tag="bank_%s%d" % (br, t))
+            banks = {}
+            for t in tile_order:
+                name = "bank_%s%d" % (branch, t)
+                banks[t] = psum.tile([P, S], F32, name=name, tag=name)
                 cols = slice(P * t, P * (t + 1))
                 nc.tensor.matmul_mx(
-                    out=bank[:], lhsT=d_dealt[:, cols].bitcast(FP8X4), lhsT_scale=planes[br][:, cols],
-                    rhs=x_picked[:].bitcast(FP8X4), rhs_scale=planes[br][:, S:], start=True, stop=True,
+                    out=banks[t][:], lhsT=d_dealt[:, cols].bitcast(FP8X4), lhsT_scale=planes[branch][:, cols],
+                    rhs=x_picked[:].bitcast(FP8X4), rhs_scale=planes[branch][:, S:], start=True, stop=True,
                 )
-                banks.append(bank)
             return banks
 
         pick_bytes("b", "k2", "two")
-        b_banks = pick_words("b", "k2", "two")
+        b_banks = pick_words_and_multiply("b", "k2", "two", range(PACK))
         pick_bytes("a", "k1", "offs")
-        a_banks = pick_words("a", "k1", "offs")
+        a_banks = pick_words_and_multiply("a", "k1", "offs", A_ORDER)
 
         gains = {}
-        for name, src, br in (("gm", gm, "b"), ("gn", gn, "a")):
-            gains[name] = keep.tile([P, PACK], F32, name=name, tag="staged_" + br, align_bytes=64)
+        for name, src, branch in (("gm", gm, "b"), ("gn", gn, "a")):
+            gains[name] = sb(name, PACK, F32, tag="staged_" + branch)
             nc.sync.dma_start(gains[name][:], src.rearrange("(p t) o -> p (t o)", t=PACK))
 
-        w_words, w_bytes, w_raw, w_raw_bytes = {}, {}, {}, {}
-        w_table = keep.tile([P, G], U8, name="w_table", tag="d_bytes", align_bytes=64)
-        w_table_bytes = keep.tile([P, T], U8, name="w_table_bytes", tag="x_bytes", align_bytes=64)
-        for k, (name, words, scales) in enumerate((("w2", w2_words, w2_scales), ("w1", w1_words, w1_scales))):
-            w_raw[name] = w_table[:, 2 * S * k : 2 * S * (k + 1)]
-            w_raw_bytes[name] = w_table_bytes[:, S * k : S * (k + 1)]
-            nc.sync.dma_start(w_raw[name].bitcast(I32), words[0].bitcast(I32))
-            nc.sync.dma_start(
-                w_raw_bytes[name].bitcast(I32), scales[0].bitcast(I32).unsqueeze(1).to_broadcast([16, 8, S // 4])
-            )
-        w_staged = sb("staged_w", 2 * S, U8)
-        for k, name in enumerate(("w2", "w1")):
-            w_words[name] = sb(name + "_dealt", 2 * S, U8)
-            w_bytes[name] = planes["w"][:, S * k : S * (k + 1)]
-            nc.vector.tensor_copy(
-                w_words[name][:].rearrange("p (t m e) -> p t m e", t=PACK, e=2),
-                w_raw[name][:].rearrange("p (m t e) -> p t m e", t=PACK, e=2),
-            )
-            nc.vector.tensor_copy(
-                w_staged[:, S * k : S * (k + 1)].rearrange("p (t m) -> p t m", t=PACK),
-                w_raw_bytes[name][:].rearrange("p (m t) -> p t m", t=PACK),
-            )
-        for i in range(4):
-            nc.sync.dma_start(planes["w"][i:P:32, :].bitcast(I32), w_staged[8 * i : P : 32, :].bitcast(I32))
-
-        z2_rows = keep.tile([P, PACK, S], BF16, name="z2_rows", align_bytes=64)
+        z2_rows = sb_rows("z2_rows", S, BF16)
         pair = [sb("pair%d" % t, S, F32) for t in range(PACK)]
         radius2 = [sb("radius2_%d" % t, HALF, F32) for t in range(PACK)]
         dt = [sb("dt%d" % t, S, F32) for t in range(PACK)]
-        gained = keep.tile([P, PACK, S], F32, name="gained", align_bytes=64)
+        gained = sb_rows("gained", S, F32)
         h_rows = [sb("h%d" % t, S, F32) for t in range(PACK)]
         z2_codes = sb("z2_codes", S, U32)
         z2_bytes = sb("z2_bytes", S, U8)
+        third = sb_rows("third", S, F32)
+        z_codes = [sb("z_codes%d" % lo, hi - lo, U32) for lo, hi in Z_PIECES]
+        z_bytes = [sb("z_bytes%d" % lo, hi - lo, U8) for lo, hi in Z_PIECES]
+        w_words, w_bytes, h_banks = {}, {}, {}
 
         def fetch_pairs(t):
             b_row = sb("b%d" % t, S, F32)
@@ -168,23 +166,44 @@ def tile_picked_pqjthreepolarwind_none_po_kernel(
             nc.vector.scalar_tensor_tensor(radius2[t][:], squares[:, :HALF], 4.0, squares[:, HALF:], ALU.mult, ALU.add)
             nc.vector.tensor_tensor(dt[t][:].indirect(lists["n5"][:]), pair[t][:, HALF:], pair[t][:, :HALF], ALU.add)
 
+        def deal_weights():
+            w_table = sb("w_table", 4 * S, U8, tag="pair%d" % (PACK - 2))
+            w_table_bytes = sb("w_table_bytes", 2 * S, U8, tag="pair%d" % (PACK - 1))
+            weights = (("w2", w2_words, w2_scales), ("w1", w1_words, w1_scales))
+            for k, (name, words, scales) in enumerate(weights):
+                nc.sync.dma_start(w_table[:, 2 * S * k : 2 * S * (k + 1)].bitcast(I32), words[0].bitcast(I32))
+                load_scale_rows(w_table_bytes[:, S * k : S * (k + 1)], scales)
+            w_staged = sb("staged_w", 2 * S, U8)
+            for k, (name, words, scales) in enumerate(weights):
+                w_words[name] = sb(name + "_dealt", 2 * S, U8)
+                w_bytes[name] = planes["w"][:, S * k : S * (k + 1)]
+                nc.gpsimd.tensor_copy(
+                    w_words[name][:].rearrange("p (t m e) -> p t m e", t=PACK, e=2),
+                    w_table[:, 2 * S * k : 2 * S * (k + 1)].rearrange("p (m t e) -> p t m e", t=PACK, e=2),
+                )
+                nc.gpsimd.tensor_copy(
+                    w_staged[:, S * k : S * (k + 1)].rearrange("p (t m) -> p t m", t=PACK),
+                    w_table_bytes[:, S * k : S * (k + 1)].rearrange("p (m t) -> p t m", t=PACK),
+                )
+            move_scale_rows(planes["w"], w_staged)
+
         def put_roots(t):
             ra = sb("ra%d" % t, HALF, F32)
             nc.scalar.activation(ra[:], radius2[t][:], ACT.Sqrt, bias=0.25)
             nc.vector.tensor_copy(dt[t][:].indirect(lists["n4"][:]), ra[:])
 
         def gain_z2(t):
-            nc.scalar.activation(z2_rows[:, t, :], dt[t][:], ACT.Copy, scale=gains["gm"][:, t : t + 1])
+            if t < GM_TILES_ON_SCALAR:
+                nc.scalar.activation(z2_rows[:, t, :], dt[t][:], ACT.Copy, scale=gains["gm"][:, t : t + 1])
+            else:
+                nc.vector.tensor_scalar(z2_rows[:, t, :], dt[t][:], gains["gm"][:, t : t + 1], None, ALU.mult)
 
         def quantise_z2():
             z2_grouped = sb("z2_grouped", PACK * S, BF16)
-            dst = z2_grouped[:].rearrange("p (g j t) -> p g t j", t=PACK, j=4)
-            src = z2_rows[:].rearrange("p t (g j) -> p g t j", j=4)
-            cut = Z2_SCALAR_COLS // 4
-            if cut:
-                nc.scalar.copy(dst[:, :cut], src[:, :cut])
-            if cut < S // 4:
-                nc.vector.tensor_copy(dst[:, cut:], src[:, cut:])
+            dst, src = grouped_view(z2_grouped[:]), rows_view(z2_rows[:])
+            cut = Z2_COLUMNS_ON_SCALAR // LINE
+            nc.scalar.copy(dst[:, :cut], src[:, :cut])
+            nc.vector.tensor_copy(dst[:, cut:], src[:, cut:])
             nc.vector.quantize_mx(out=z2_codes[:].bitcast(FP8X4), scales=z2_bytes[:], in_=z2_grouped[:])
 
         def less_first(t):
@@ -198,95 +217,91 @@ def tile_picked_pqjthreepolarwind_none_po_kernel(
             su = sb("su%d" % t, S, F32)
             nc.scalar.activation(second[:], st_rows[t][:].indirect(lists["n2"][:]), ACT.Copy)
             nc.vector.tensor_tensor(su[:], st_rows[t][:, :S], second[:], ALU.max)
-            if t in GAIN_ON_SCALAR:
-                nc.scalar.activation(gained[:, t, :], su[:], ACT.Copy, scale=gains["gn"][:, t : t + 1])
-            else:
-                nc.vector.tensor_scalar(gained[:, t, :], su[:], gains["gn"][:, t : t + 1], None, ALU.mult)
+            nc.vector.tensor_scalar(gained[:, t, :], su[:], gains["gn"][:, t : t + 1], None, ALU.mult)
 
-        def make_z(c):
-            lo, hi = Z_PIECES[c]
-            width = hi - lo
-            third = keep.tile([P, PACK, width], F32, name="third%d" % c, align_bytes=64)
-            for t in range(PACK):
-                nc.scalar.activation(
-                    third[:, t, :], gained[:, t, :].indirect(lists["n3"][:, lo // 16 : hi // 16]), ACT.Copy, scale=0.5
-                )
-            z_grouped = sb("z_grouped%d" % c, PACK * width, BF16)
+        def fetch_third(piece):
+            lo, hi = Z_PIECES[piece]
+            entries = lists["n3"][:, lo // LIST_ROWS : hi // LIST_ROWS]
+            for t in range(1, PACK):
+                nc.scalar.activation(third[:, t, lo:hi], gained[:, t, :].indirect(entries), ACT.Copy, scale=0.5)
+
+        def fetch_third_of_tile_0():
+            whole = gained[:].rearrange("p t j -> p (t j)")
+            nc.vector.tensor_scalar(third[:, 0, :], whole.indirect(lists["n3"][:]), 0.5, 0.0, ALU.mult, ALU.add)
+
+        def quantise_z(piece):
+            lo, hi = Z_PIECES[piece]
+            z_grouped = sb("z_grouped%d" % piece, PACK * (hi - lo), BF16, tag="z_grouped")
             nc.vector.tensor_tensor(
-                z_grouped[:].rearrange("p (g j t) -> p g t j", t=PACK, j=4),
-                third[:].rearrange("p t (g j) -> p g t j", j=4),
-                gained[:, :, lo:hi].rearrange("p t (g j) -> p g t j", j=4),
-                ALU.add,
+                grouped_view(z_grouped[:]), rows_view(third[:, :, lo:hi]), rows_view(gained[:, :, lo:hi]), ALU.add
             )
-            z_codes = sb("z_codes%d" % c, width, U32)
-            z_bytes = sb("z_bytes%d" % c, width, U8)
-            nc.vector.quantize_mx(out=z_codes[:].bitcast(FP8X4), scales=z_bytes[:], in_=z_grouped[:])
-            return z_codes, z_bytes
+            nc.vector.quantize_mx(out=z_codes[piece][:].bitcast(FP8X4), scales=z_bytes[piece][:], in_=z_grouped[:])
 
-        def sum_h(c, z_codes, z_bytes):
-            lo, hi = Z_PIECES[c]
-            cols = slice(lo, hi)
-            banks = [
-                psum.tile([P, hi - lo], F32, name="bank_h%d_%d" % (t, c), tag="bank_%s%d" % ("ba"[c % 2], t)) for t in range(PACK)
-            ]
-            for name, codes, scale_bytes in (
-                ("w2", z2_codes[:, cols], z2_bytes[:, cols]), ("w1", z_codes[:], z_bytes[:])
-            ):
+        def weight_pass(name, piece, t, codes, scale_bytes):
+            nc.tensor.matmul_mx(
+                out=h_banks[piece, t][:], lhsT=w_words[name][:, 2 * P * t : 2 * P * (t + 1)].bitcast(FP4X4),
+                lhsT_scale=w_bytes[name][:, P * t : P * (t + 1)],
+                rhs=codes.bitcast(FP8X4), rhs_scale=scale_bytes, start=(name == "w2"), stop=(name == "w1"),
+            )
+
+        def open_h():
+            for piece, (lo, hi) in enumerate(Z_PIECES):
                 for t in range(PACK):
-                    nc.tensor.matmul_mx(
-                        out=banks[t][:], lhsT=w_words[name][:, 2 * P * t : 2 * P * (t + 1)].bitcast(FP4X4),
-                        lhsT_scale=w_bytes[name][:, P * t : P * (t + 1)],
-                        rhs=codes.bitcast(FP8X4), rhs_scale=scale_bytes, start=(name == "w2"), stop=(name == "w1"),
+                    h_banks[piece, t] = psum.tile(
+                        [P, hi - lo], F32, name="bank_h%d_%d" % (t, piece), tag="bank_%s%d" % ("ba"[piece], t)
                     )
+                    weight_pass("w2", piece, t, z2_codes[:, lo:hi], z2_bytes[:, lo:hi])
+
+        def close_h(piece, copy_out):
+            lo, hi = Z_PIECES[piece]
             for t in range(PACK):
-                if (c, t) in H_ON_VECTOR:
-                    nc.vector.tensor_copy(h_rows[t][:, cols], banks[t][:])
-                else:
-                    nc.scalar.copy(h_rows[t][:, cols], banks[t][:])
+                weight_pass("w1", piece, t, z_codes[piece][:], z_bytes[piece][:])
+            for t in range(PACK):
+                copy_out(h_rows[t][:, lo:hi], h_banks[piece, t][:])
 
         for t in range(PACK):
             fetch_pairs(t)
+        deal_weights()
         for t in range(PACK):
-            less_first(t)
+            less_first(A_ORDER[t])
             put_roots(t)
         for t in range(PACK):
-            larger_of_second(t)
+            larger_of_second(A_ORDER[t])
             gain_z2(t)
         quantise_z2()
-        for c in range(len(Z_PIECES)):
-            sum_h(c, *make_z(c))
+        open_h()
+        fetch_third(0)
+        fetch_third_of_tile_0()
+        quantise_z(0)
+        close_h(0, nc.scalar.copy)
+        fetch_third(1)
+        quantise_z(1)
+        close_h(1, nc.vector.tensor_copy)
+
         out_rows = out_0.rearrange("(p t) j -> p t j", t=PACK)
         out_words = out_1[0].rearrange("p n r -> p (n r)").bitcast(I32)
         y_bytes = sb("y_bytes", S, U8)
-        for c, (lo, hi) in enumerate(Y_PIECES):
-            cols = slice(lo, hi)
+        for piece, (lo, hi) in enumerate(Y_PIECES):
             width = hi - lo
-            entries = slice(lo // 16, hi // 16)
-            y_rows = keep.tile([P, PACK, width], F32, name="y_rows%d" % c, align_bytes=64)
+            entries = slice(lo // LIST_ROWS, hi // LIST_ROWS)
+            y_rows = sb_rows("y_rows%d" % piece, width, F32)
             for t in range(PACK):
-                seventh = sb("seventh%d_%d" % (t, c), width, F32)
-                diff = sb("diff%d_%d" % (t, c), width, F32)
+                seventh = sb("seventh%d_%d" % (t, piece), width, F32)
+                diff = sb("diff%d_%d" % (t, piece), width, F32)
                 nc.scalar.activation(seventh[:], h_rows[t][:].indirect(lists["n7"][:, entries]), ACT.Copy, scale=-1.0)
-                if (c, t) not in SIXTH_ON_SCALAR:
-                    nc.vector.tensor_tensor(diff[:], h_rows[t][:].indirect(lists["n6"][:, entries]), seventh[:], ALU.add)
-                else:
-                    sixth = sb("sixth%d_%d" % (t, c), width, F32)
+                if piece == 0 and t == PACK - 1:
+                    sixth = sb("sixth", width, F32)
                     nc.scalar.activation(sixth[:], h_rows[t][:].indirect(lists["n6"][:, entries]), ACT.Copy)
                     nc.vector.tensor_tensor(diff[:], sixth[:], seventh[:], ALU.add)
-                nc.vector.tensor_tensor(y_rows[:, t, :], diff[:], h_rows[t][:, cols], ALU.mult)
-            nc.sync.dma_start(out_rows[:, :, cols], y_rows[:])
-            y_grouped = sb("y_grouped%d" % c, PACK * width, BF16)
-            y_codes = sb("y_codes%d" % c, width, U32)
-            if c in Y_GROUP_ON_SCALAR:
-                nc.scalar.copy(
-                    y_grouped[:].rearrange("p (g j t) -> p g t j", t=PACK, j=4), y_rows[:].rearrange("p t (g j) -> p g t j", j=4)
-                )
-            else:
-                nc.vector.tensor_copy(
-                    y_grouped[:].rearrange("p (g j t) -> p g t j", t=PACK, j=4), y_rows[:].rearrange("p t (g j) -> p g t j", j=4)
-                )
-            nc.vector.quantize_mx(out=y_codes[:].bitcast(FP8X4), scales=y_bytes[:, cols], in_=y_grouped[:])
-            nc.sync.dma_start(out_words[:, cols], y_codes[:].bitcast(I32))
+                else:
+                    nc.vector.tensor_tensor(diff[:], h_rows[t][:].indirect(lists["n6"][:, entries]), seventh[:], ALU.add)
+                nc.vector.tensor_tensor(y_rows[:, t, :], diff[:], h_rows[t][:, lo:hi], ALU.mult)
+            nc.sync.dma_start(out_rows[:, :, lo:hi], y_rows[:])
+            y_grouped = sb("y_grouped%d" % piece, PACK * width, BF16)
+            y_codes = sb("y_codes%d" % piece, width, U32)
+            nc.scalar.copy(grouped_view(y_grouped[:]), rows_view(y_rows[:]))
+            nc.vector.quantize_mx(out=y_codes[:].bitcast(FP8X4), scales=y_bytes[:, lo:hi], in_=y_grouped[:])
+            nc.sync.dma_start(out_words[:, lo:hi], y_codes[:].bitcast(I32))
         for q in range(4):
             queue = nc.sync if q % 2 == 0 else nc.scalar
             queue.dma_start(out_2[0, 4 * q : 4 * q + 4, :].bitcast(I32), y_bytes[32 * q : 32 * q + 4, :].bitcast(I32))

from contextlib import ExitStack

import concourse.mybir as mybir

F32 = mybir.dt.float32
BF16 = mybir.dt.bfloat16
I32 = mybir.dt.int32
U32 = mybir.dt.uint32
U16 = mybir.dt.uint16
U8 = mybir.dt.uint8
FP8X4 = mybir.dt.float8_e4m3fn_x4
FP4X4 = mybir.dt.float4_e2m1fn_x4
ALU = mybir.AluOpType
ACT = mybir.ActivationFunctionType

P = 128
PACK = 4
S = 512
HALF = S // 2
PAD = 8
T = 1024
G = 2048
LIST_ROWS = 16
LINE = 4

Z_PIECES = ((0, HALF), (HALF, S))
Y_PIECES = ((0, 384), (384, S))
A_ORDER = (1, 2, 3, 0)
GM_TILES_ON_SCALAR = 2
Z2_COLUMNS_ON_SCALAR = 256

FLOPS = 4 * 2 * 512 * 512 * 512


def tile_picked_pqjthreepolarwind_none_po_kernel(
    tc, x_words, x_scales, d_words, d_scales, gn, gm, w1_words, w1_scales, w2_words, w2_scales,
    offs, k1, two, k2, n1, n2, n3, n4, n5, n6, n7, out_0, out_1, out_2,
):
    nc = tc.nc
    with ExitStack() as ctx:
        keep = ctx.enter_context(tc.tile_pool(name="keep", bufs=1))
        psum = ctx.enter_context(tc.psum_pool(name="psum", bufs=1))

        def sb(name, cols, dtype, tag=None):
            return keep.tile([P, cols], dtype, name=name, tag=tag or name, align_bytes=64)

        def sb_rows(name, cols, dtype):
            return keep.tile([P, PACK, cols], dtype, name=name, align_bytes=64)

        def grouped_view(tile):
            return tile.rearrange("p (g j t) -> p g t j", t=PACK, j=LINE)

        def rows_view(rows):
            return rows.rearrange("p t (g j) -> p g t j", j=LINE)

        def load_scale_rows(tile, scales):
            rows = scales[0].bitcast(I32)
            nc.sync.dma_start(tile.bitcast(I32), rows.unsqueeze(1).to_broadcast([16, 8, rows.shape[1]]))

        def move_scale_rows(plane, staged):
            for i in range(4):
                nc.sync.dma_start(plane[i:P:32, :].bitcast(I32), staged[8 * i : P : 32, :].bitcast(I32))

        lists = {}

        def load_list(name, src):
            lists[name] = keep.tile([P, src.shape[1]], U16, name="list_" + name)
            nc.sync.dma_start(lists[name][:], src)

        d_bytes = sb("d_bytes", G, U8)
        x_bytes = sb("x_bytes", T, U8)
        load_list("k2", k2)
        load_scale_rows(d_bytes[:], d_scales)
        load_list("two", two)
        load_scale_rows(x_bytes[:], x_scales)
        x_table = sb("x_table", T, I32)
        d_table = sb("d_table", G, I32)
        nc.sync.dma_start(d_table[:], d_words[0].rearrange("p n r -> p (n r)").bitcast(I32))
        nc.sync.dma_start(x_table[:], x_words[0].rearrange("p n r -> p (n r)").bitcast(I32))
        for name, src in (
            ("n4", n4), ("n5", n5), ("k1", k1), ("offs", offs),
            ("n1", n1), ("n2", n2), ("n3", n3), ("n6", n6), ("n7", n7),
        ):
            load_list(name, src)

        warm = sb("warm", 2, F32)
        nc.vector.memset(warm[:, :1], 1.0)
        nc.scalar.activation(warm[:, 1:], warm[:, :1], ACT.Sqrt)

        planes = {}
        for name in ("b", "a", "w"):
            planes[name] = sb("plane_" + name, 2 * S, U8)
            nc.vector.memset(planes[name][:].bitcast(I32), 0)

        def padded(name):
            tile = sb(name, S + PAD, F32)
            nc.vector.memset(tile[:, S:], 0.0)
            return tile

        a_rows = [padded("a%d" % t) for t in range(PACK)]
        st_rows = [padded("st%d" % t) for t in range(PACK)]

        def pick_bytes(branch, d_list, x_list):
            d_picked = sb("d_picked_bytes_" + branch, S, U8)
            x_picked = sb("x_picked_bytes_" + branch, S, U8)
            staged = sb("staged_" + branch, 2 * S, U8)
            nc.vector.tensor_copy(d_picked[:], d_bytes[:].indirect(lists[d_list][:]))
            nc.vector.tensor_copy(x_picked[:], x_bytes[:].indirect(lists[x_list][:]))
            nc.vector.tensor_copy(
                staged[:, :S].rearrange("p (t m) -> p t m", t=PACK), d_picked[:].rearrange("p (m t) -> p t m", t=PACK)
            )
            nc.vector.tensor_copy(staged[:, S:].bitcast(I32), x_picked[:].bitcast(I32))
            move_scale_rows(planes[branch], staged)

        def pick_words_and_multiply(branch, d_list, x_list, tile_order):
            x_picked = sb("x_picked_" + branch, S, U32)
            d_picked = sb("d_picked_" + branch, S, U32)
            d_dealt = sb("d_dealt_" + branch, S, U32)
            nc.vector.tensor_copy(d_picked[:], d_table[:].bitcast(U32).indirect(lists[d_list][:]))
            nc.vector.tensor_copy(x_picked[:], x_table[:].bitcast(U32).indirect(lists[x_list][:]))
            nc.vector.tensor_copy(
                d_dealt[:].bitcast(I32).rearrange("p (t g m) -> p g t m", t=PACK, m=LINE),
                d_picked[:].bitcast(I32).rearrange("p (g m t) -> p g t m", t=PACK, m=LINE),
            )
            banks = {}
            for t in tile_order:
                name = "bank_%s%d" % (branch, t)
                banks[t] = psum.tile([P, S], F32, name=name, tag=name)
                cols = slice(P * t, P * (t + 1))
                nc.tensor.matmul_mx(
                    out=banks[t][:], lhsT=d_dealt[:, cols].bitcast(FP8X4), lhsT_scale=planes[branch][:, cols],
                    rhs=x_picked[:].bitcast(FP8X4), rhs_scale=planes[branch][:, S:], start=True, stop=True,
                )
            return banks

        pick_bytes("b", "k2", "two")
        b_banks = pick_words_and_multiply("b", "k2", "two", range(PACK))
        pick_bytes("a", "k1", "offs")
        a_banks = pick_words_and_multiply("a", "k1", "offs", A_ORDER)

        gains = {}
        for name, src, branch in (("gm", gm, "b"), ("gn", gn, "a")):
            gains[name] = sb(name, PACK, F32, tag="staged_" + branch)
            nc.sync.dma_start(gains[name][:], src.rearrange("(p t) o -> p (t o)", t=PACK))

        z2_rows = sb_rows("z2_rows", S, BF16)
        pair = [sb("pair%d" % t, S, F32) for t in range(PACK)]
        radius2 = [sb("radius2_%d" % t, HALF, F32) for t in range(PACK)]
        dt = [sb("dt%d" % t, S, F32) for t in range(PACK)]
        gained = sb_rows("gained", S, F32)
        h_rows = [sb("h%d" % t, S, F32) for t in range(PACK)]
        z2_codes = sb("z2_codes", S, U32)
        z2_bytes = sb("z2_bytes", S, U8)
        third = sb_rows("third", S, F32)
        z_codes = [sb("z_codes%d" % lo, hi - lo, U32) for lo, hi in Z_PIECES]
        z_bytes = [sb("z_bytes%d" % lo, hi - lo, U8) for lo, hi in Z_PIECES]
        w_words, w_bytes, h_banks = {}, {}, {}

        def fetch_pairs(t):
            b_row = sb("b%d" % t, S, F32)
            squares = sb("squares%d" % t, S, F32)
            nc.scalar.activation(b_row[:], b_banks[t][:], ACT.Copy, scale=0.0625)
            nc.scalar.activation(pair[t][:, :HALF], b_row[:].indirect(lists["n4"][:]), ACT.Copy, scale=-0.5)
            nc.scalar.activation(pair[t][:, HALF:], b_row[:].indirect(lists["n5"][:]), ACT.Copy)
            nc.scalar.activation(squares[:], pair[t][:], ACT.Square)
            nc.vector.scalar_tensor_tensor(radius2[t][:], squares[:, :HALF], 4.0, squares[:, HALF:], ALU.mult, ALU.add)
            nc.vector.tensor_tensor(dt[t][:].indirect(lists["n5"][:]), pair[t][:, HALF:], pair[t][:, :HALF], ALU.add)

        def deal_weights():
            w_table = sb("w_table", 4 * S, U8, tag="pair%d" % (PACK - 2))
            w_table_bytes = sb("w_table_bytes", 2 * S, U8, tag="pair%d" % (PACK - 1))
            weights = (("w2", w2_words, w2_scales), ("w1", w1_words, w1_scales))
            for k, (name, words, scales) in enumerate(weights):
                nc.sync.dma_start(w_table[:, 2 * S * k : 2 * S * (k + 1)].bitcast(I32), words[0].bitcast(I32))
                load_scale_rows(w_table_bytes[:, S * k : S * (k + 1)], scales)
            w_staged = sb("staged_w", 2 * S, U8)
            for k, (name, words, scales) in enumerate(weights):
                w_words[name] = sb(name + "_dealt", 2 * S, U8)
                w_bytes[name] = planes["w"][:, S * k : S * (k + 1)]
                nc.gpsimd.tensor_copy(
                    w_words[name][:].rearrange("p (t m e) -> p t m e", t=PACK, e=2),
                    w_table[:, 2 * S * k : 2 * S * (k + 1)].rearrange("p (m t e) -> p t m e", t=PACK, e=2),
                )
                nc.gpsimd.tensor_copy(
                    w_staged[:, S * k : S * (k + 1)].rearrange("p (t m) -> p t m", t=PACK),
                    w_table_bytes[:, S * k : S * (k + 1)].rearrange("p (m t) -> p t m", t=PACK),
                )
            move_scale_rows(planes["w"], w_staged)

        def put_roots(t):
            ra = sb("ra%d" % t, HALF, F32)
            nc.scalar.activation(ra[:], radius2[t][:], ACT.Sqrt, bias=0.25)
            nc.vector.tensor_copy(dt[t][:].indirect(lists["n4"][:]), ra[:])

        def gain_z2(t):
            if t < GM_TILES_ON_SCALAR:
                nc.scalar.activation(z2_rows[:, t, :], dt[t][:], ACT.Copy, scale=gains["gm"][:, t : t + 1])
            else:
                nc.vector.tensor_scalar(z2_rows[:, t, :], dt[t][:], gains["gm"][:, t : t + 1], None, ALU.mult)

        def quantise_z2():
            z2_grouped = sb("z2_grouped", PACK * S, BF16)
            dst, src = grouped_view(z2_grouped[:]), rows_view(z2_rows[:])
            cut = Z2_COLUMNS_ON_SCALAR // LINE
            nc.scalar.copy(dst[:, :cut], src[:, :cut])
            nc.vector.tensor_copy(dst[:, cut:], src[:, cut:])
            nc.vector.quantize_mx(out=z2_codes[:].bitcast(FP8X4), scales=z2_bytes[:], in_=z2_grouped[:])

        def less_first(t):
            first = sb("first%d" % t, S, F32)
            nc.scalar.activation(a_rows[t][:, :S], a_banks[t][:], ACT.Copy, scale=0.0625)
            nc.scalar.activation(first[:], a_rows[t][:].indirect(lists["n1"][:]), ACT.Copy)
            nc.vector.scalar_tensor_tensor(st_rows[t][:, :S], a_banks[t][:], 0.0625, first[:], ALU.mult, ALU.subtract)

        def larger_of_second(t):
            second = sb("second%d" % t, S, F32)
            su = sb("su%d" % t, S, F32)
            nc.scalar.activation(second[:], st_rows[t][:].indirect(lists["n2"][:]), ACT.Copy)
            nc.vector.tensor_tensor(su[:], st_rows[t][:, :S], second[:], ALU.max)
            nc.vector.tensor_scalar(gained[:, t, :], su[:], gains["gn"][:, t : t + 1], None, ALU.mult)

        def fetch_third(piece):
            lo, hi = Z_PIECES[piece]
            entries = lists["n3"][:, lo // LIST_ROWS : hi // LIST_ROWS]
            for t in range(1, PACK):
                nc.scalar.activation(third[:, t, lo:hi], gained[:, t, :].indirect(entries), ACT.Copy, scale=0.5)

        def fetch_third_of_tile_0():
            whole = gained[:].rearrange("p t j -> p (t j)")
            nc.vector.tensor_scalar(third[:, 0, :], whole.indirect(lists["n3"][:]), 0.5, 0.0, ALU.mult, ALU.add)

        def quantise_z(piece):
            lo, hi = Z_PIECES[piece]
            z_grouped = sb("z_grouped%d" % piece, PACK * (hi - lo), BF16, tag="z_grouped")
            nc.vector.tensor_tensor(
                grouped_view(z_grouped[:]), rows_view(third[:, :, lo:hi]), rows_view(gained[:, :, lo:hi]), ALU.add
            )
            nc.vector.quantize_mx(out=z_codes[piece][:].bitcast(FP8X4), scales=z_bytes[piece][:], in_=z_grouped[:])

        def weight_pass(name, piece, t, codes, scale_bytes):
            nc.tensor.matmul_mx(
                out=h_banks[piece, t][:], lhsT=w_words[name][:, 2 * P * t : 2 * P * (t + 1)].bitcast(FP4X4),
                lhsT_scale=w_bytes[name][:, P * t : P * (t + 1)],
                rhs=codes.bitcast(FP8X4), rhs_scale=scale_bytes, start=(name == "w2"), stop=(name == "w1"),
            )

        def open_h():
            for piece, (lo, hi) in enumerate(Z_PIECES):
                for t in range(PACK):
                    h_banks[piece, t] = psum.tile(
                        [P, hi - lo], F32, name="bank_h%d_%d" % (t, piece), tag="bank_%s%d" % ("ba"[piece], t)
                    )
                    weight_pass("w2", piece, t, z2_codes[:, lo:hi], z2_bytes[:, lo:hi])

        def close_h(piece, copy_out):
            lo, hi = Z_PIECES[piece]
            for t in range(PACK):
                weight_pass("w1", piece, t, z_codes[piece][:], z_bytes[piece][:])
            for t in range(PACK):
                copy_out(h_rows[t][:, lo:hi], h_banks[piece, t][:])

        for t in range(PACK):
            fetch_pairs(t)
        deal_weights()
        for t in range(PACK):
            less_first(A_ORDER[t])
            put_roots(t)
        for t in range(PACK):
            larger_of_second(A_ORDER[t])
            gain_z2(t)
        quantise_z2()
        open_h()
        fetch_third(0)
        fetch_third_of_tile_0()
        quantise_z(0)
        close_h(0, nc.scalar.copy)
        fetch_third(1)
        quantise_z(1)
        close_h(1, nc.vector.tensor_copy)

        out_rows = out_0.rearrange("(p t) j -> p t j", t=PACK)
        out_words = out_1[0].rearrange("p n r -> p (n r)").bitcast(I32)
        y_bytes = sb("y_bytes", S, U8)
        for piece, (lo, hi) in enumerate(Y_PIECES):
            width = hi - lo
            entries = slice(lo // LIST_ROWS, hi // LIST_ROWS)
            y_rows = sb_rows("y_rows%d" % piece, width, F32)
            for t in range(PACK):
                seventh = sb("seventh%d_%d" % (t, piece), width, F32)
                diff = sb("diff%d_%d" % (t, piece), width, F32)
                nc.scalar.activation(seventh[:], h_rows[t][:].indirect(lists["n7"][:, entries]), ACT.Copy, scale=-1.0)
                if piece == 0 and t == PACK - 1:
                    sixth = sb("sixth", width, F32)
                    nc.scalar.activation(sixth[:], h_rows[t][:].indirect(lists["n6"][:, entries]), ACT.Copy)
                    nc.vector.tensor_tensor(diff[:], sixth[:], seventh[:], ALU.add)
                else:
                    nc.vector.tensor_tensor(diff[:], h_rows[t][:].indirect(lists["n6"][:, entries]), seventh[:], ALU.add)
                nc.vector.tensor_tensor(y_rows[:, t, :], diff[:], h_rows[t][:, lo:hi], ALU.mult)
            nc.sync.dma_start(out_rows[:, :, lo:hi], y_rows[:])
            y_grouped = sb("y_grouped%d" % piece, PACK * width, BF16)
            y_codes = sb("y_codes%d" % piece, width, U32)
            nc.scalar.copy(grouped_view(y_grouped[:]), rows_view(y_rows[:]))
            nc.vector.quantize_mx(out=y_codes[:].bitcast(FP8X4), scales=y_bytes[:, lo:hi], in_=y_grouped[:])
            nc.sync.dma_start(out_words[:, lo:hi], y_codes[:].bitcast(I32))
        for q in range(4):
            queue = nc.sync if q % 2 == 0 else nc.scalar
            queue.dma_start(out_2[0, 4 * q : 4 * q + 4, :].bitcast(I32), y_bytes[32 * q : 32 * q + 4, :].bitcast(I32))
